import numpy as np
import ml_dtypes


def mxq(x, axis, fmt="e4m3"):
    dtype, down = {"e4m3": (ml_dtypes.float8_e4m3fn, 7), "e5m2": (ml_dtypes.float8_e5m2, 14)}[fmt]
    v = np.moveaxis(np.asarray(x, np.float32).astype(ml_dtypes.bfloat16).astype(np.float64), axis, -1)
    blocks = v.reshape(v.shape[:-1] + (-1, 32))
    amax = np.abs(blocks).max(-1, keepdims=True)
    byte = np.maximum(np.where(amax > 0, np.frexp(amax)[1] - 1 + 127, 0) - down, 1)
    scale = np.exp2(byte - 127.0)
    codes = (blocks / scale).astype(np.float32).astype(dtype).astype(np.float64)
    return np.moveaxis((codes * scale).reshape(v.shape), -1, axis)


WIDE = False


def mx_kscale(k):
    if not WIDE:
        return np.ones(k)
    levels = np.array([30, -30])
    if k % 512:
        return np.exp2(np.random.permutation(np.resize(levels, k // 32))).repeat(32)
    a = np.empty((k // 512, 16))
    for p in range(k // 512):
        a[p, :8] = np.random.permutation(np.resize(levels, 8))
        for g in range(8):
            far = levels[np.abs(levels - a[p, g]) >= 10]
            a[p, g + 8] = far[np.random.randint(len(far))]
    return np.exp2(a.ravel()).repeat(32)


def f64(x):
    return np.asarray(x).astype(np.float64)


def striped(idx):
    return np.tile(np.asarray(idx).reshape(-1, 16).T, (8, 1)).astype(np.uint16)


def unstriped(offs):
    return offs[:16].T.reshape(-1).astype(np.int64)


E2M1 = np.array([0.0, 0.5, 1.0, 1.5, 2.0, 3.0, 4.0, 6.0, -0.0, -0.5, -1.0, -1.5, -2.0, -3.0, -4.0, -6.0])


def pack_weight(w, fmt):
    k, n = w.shape
    w = f64(np.asarray(w, np.float32).astype(ml_dtypes.bfloat16)).reshape(k // 32, 32, n)
    amax = np.abs(w).max(1)
    if fmt in ("e4m3", "e5m2"):
        byte = np.frexp(amax)[1] - 1 + 127 - (7 if fmt == "e4m3" else 14)
    else:
        mant, ex = np.frexp(amax / 6.0)
        byte = np.where(mant > 0.5, ex, ex - 1) + 127
    byte = np.clip(np.where(amax > 0, byte, 1), 1, 254)
    scaled = (w * np.exp2(127.0 - byte)[:, None, :]).reshape(k, n).astype(np.float32)
    by_word = np.ascontiguousarray(scaled.reshape(k // 512, 128, 4, n).transpose(0, 1, 3, 2))
    if fmt in ("e4m3", "e5m2"):
        words = by_word.astype(ml_dtypes.float8_e4m3fn if fmt == "e4m3" else ml_dtypes.float8_e5m2).view(np.uint8)
    else:
        c = by_word.astype(ml_dtypes.float4_e2m1fn).view(np.uint8) & 0xF
        words = (c[..., 0::2] | (c[..., 1::2] << 4)).reshape(k // 512, 128, 2 * n)
    return np.ascontiguousarray(words), np.ascontiguousarray(byte.astype(np.uint8).reshape(k // 512, 16, n))


def unpack_weight(words, scales, fmt):
    g, _, n = scales.shape
    words = np.ascontiguousarray(words).reshape(g, 128, n, -1)
    if fmt in ("e4m3", "e5m2"):
        vals = words.view(ml_dtypes.float8_e4m3fn if fmt == "e4m3" else ml_dtypes.float8_e5m2).astype(np.float64)
    else:
        nib = np.empty((g, 128, n, 4), np.uint8)
        nib[..., 0::2] = words & 0xF
        nib[..., 1::2] = words >> 4
        vals = E2M1[nib]
    vals = vals * np.repeat(np.exp2(scales.astype(np.float64) - 127.0), 8, axis=1)[..., None]
    return vals.transpose(0, 1, 3, 2).reshape(g * 512, n)


K, T, J, S, R, F, N, C = 512, 512, 256, 512, 512, 512, 256, 1024


def setup_inputs():
    n = np.random.standard_normal
    idx = np.random.permutation(T)[:J]
    idx2 = np.random.permutation(S)[:J]
    idx3 = np.random.permutation(C)[:J]
    fk = mx_kscale(K)
    fr = mx_kscale(R)
    ff = mx_kscale(F)
    wp = pack_weight(n((K, R)) * 1 / np.sqrt(K) * fk[:, None] * fr, "e2m1")
    sxp = pack_weight(n((F, J)) / ff[:, None], "e4m3")
    w2p = pack_weight(n((F, R)) * 1 / np.sqrt(F) * ff[:, None] * fr, "e5m2")
    wbp = pack_weight(n((R, N)) * 1 / np.sqrt(R) / fr[:, None], "e5m2")
    return {
        "xa": (n((K, T))).astype(np.float32),
        "xb": (n((K, S))).astype(np.float32),
        "fk": (np.random.uniform(0.5, 2.0, (K, 1)) / fk[:, None]).astype(np.float32),
        "w_words": wp[0],
        "w_scales": wp[1],
        "sx_words": sxp[0],
        "sx_scales": sxp[1],
        "w2_words": w2p[0],
        "w2_scales": w2p[1],
        "wb_words": wbp[0],
        "wb_scales": wbp[1],
        "old": (1.0 * n((N, C))).astype(np.float32),
        "offs": striped(idx),
        "offs2": striped(idx2),
        "offs3": striped(idx3),
    }


def reference(xa, xb, fk, w_words, w_scales, sx_words, sx_scales, w2_words, w2_scales, wb_words, wb_scales, old, offs, offs2, offs3):
    idx = unstriped(offs)
    idx2 = unstriped(offs2)
    idx3 = unstriped(offs3)
    wu = unpack_weight(w_words, w_scales, "e2m1")
    sxu = unpack_weight(sx_words, sx_scales, "e4m3")
    w2u = unpack_weight(w2_words, w2_scales, "e5m2")
    wbu = unpack_weight(wb_words, wb_scales, "e5m2")
    u = f64(xa)[:, idx] * f64(xb)[:, idx2] * f64(fk)
    uq = mxq(u, 0, "e4m3")
    a = wu.T @ uq
    q = w2u.T @ sxu
    hid = np.maximum(a, 0.0) - 0.5 * np.minimum(a, q)
    hidq = mxq(hid, 0, "e5m2")
    p = wbu.T @ hidq
    pp = np.zeros((N, C))
    pp[:, idx3] = p
    y = pp + 0.5 * f64(old)
    return y

@@ -1,0 +1,208 @@
+from contextlib import ExitStack
+
+import concourse.mybir as mybir
+
+K, T, J, S, R, F, N, C = 512, 512, 256, 512, 512, 512, 256, 1024
+FLOPS = 2 * (K * R * J + F * R * J + R * N * J)
+
+F32 = mybir.dt.float32
+BF16 = mybir.dt.bfloat16
+I32 = mybir.dt.int32
+U32 = mybir.dt.uint32
+U16 = mybir.dt.uint16
+U8 = mybir.dt.uint8
+E4M3 = mybir.dt.float8_e4m3fn_x4
+E5M2 = mybir.dt.float8_e5m2_x4
+E2M1 = mybir.dt.float4_e2m1fn_x4
+ALU = mybir.AluOpType
+COPY = mybir.ActivationFunctionType.Copy
+
+P = 128
+PACK = 4
+HALF = J // 2
+LIST_COLS = HALF // 16
+OUT_CHUNK = 512
+
+ROW = R + J
+W_SC, SX_SC, W2_SC, WB_SC = 0, R, ROW, ROW + R
+
+
+def tile_list_two_entryproducts_own_smaller_scattered_kernel(
+    tc, xa, xb, fk, w_words, w_scales, sx_words, sx_scales, w2_words, w2_scales,
+    wb_words, wb_scales, old, offs, offs2, offs3, out,
+):
+    nc = tc.nc
+    with ExitStack() as ctx:
+        keep = ctx.enter_context(tc.tile_pool(name="keep", bufs=1))
+        psum = ctx.enter_context(tc.psum_pool(name="psum", bufs=1))
+
+        scales = keep.tile([P, 2 * ROW], U8, name="scales", align_bytes=64)
+        landed = keep.tile([P, ROW + R], U8, name="landed", align_bytes=64)
+        nc.scalar.dma_start(out=landed[0:32:2, ROW:].bitcast(I32), in_=w_scales[0].bitcast(I32))
+        nc.scalar.dma_start(out=landed[1:32:2, ROW:].bitcast(I32), in_=w2_scales[0].bitcast(I32))
+        nc.scalar.dma_start(out=landed[0:32:2, R:ROW].bitcast(I32), in_=sx_scales[0].bitcast(I32))
+        nc.scalar.dma_start(out=landed[1:32:2, R:ROW].bitcast(I32), in_=wb_scales[0].bitcast(I32))
+        nc.vector.memset(landed[32:64, ROW:].bitcast(I32), 0)
+        nc.vector.memset(landed[64:128, ROW:].bitcast(I32), 0)
+        nc.vector.memset(scales[:].bitcast(I32), 0)
+        fk_sb = keep.tile([P, PACK], F32, name="fk_sb")
+        nc.gpsimd.dma_start(out=fk_sb[:], in_=fk.rearrange("(p t) o -> p (t o)", t=PACK))
+
+        list_a = keep.tile([P, J // 16], U16, name="list_a")
+        list_b = keep.tile([P, J // 16], U16, name="list_b")
+        list_c = keep.tile([P, J // 16], U16, name="list_c")
+        w_raw = keep.tile([P, 2 * R], U8, name="w_raw", tag="words0", align_bytes=64)
+        w2_raw = keep.tile([P, R], U32, name="w2_raw", tag="words1", align_bytes=64)
+        xa_rows = xa.rearrange("(p t) c -> p (t c)", t=PACK)
+        xb_rows = xb.rearrange("(p t) c -> p (t c)", t=PACK)
+        xa_sb = [keep.tile([P, 2 * T], F32, name="xa%d" % i, tag="page%d" % i) for i in range(2)]
+        xb_sb = [keep.tile([P, S], F32, name="xb%d" % t, tag="late%d" % t, align_bytes=64) for t in range(2)]
+
+        def words(ap):
+            return ap[0].rearrange("p n t -> p (n t)").bitcast(I32)
+
+        nc.sync.dma_start(list_a[:], offs)
+        nc.sync.dma_start(out=w_raw[:].bitcast(I32), in_=w_words[0].bitcast(I32))
+        nc.sync.dma_start(out=w2_raw[:].bitcast(I32), in_=words(w2_words))
+        nc.sync.dma_start(out=xa_sb[0][:], in_=xa_rows[:, 0 : 2 * T])
+        nc.sync.dma_start(list_b[:], offs2)
+        nc.sync.dma_start(out=xb_sb[0][:], in_=xb_rows[:, 0:S])
+        nc.sync.dma_start(out=xa_sb[1][:], in_=xa_rows[:, 2 * T : 4 * T])
+        nc.sync.dma_start(out=xb_sb[1][:], in_=xb_rows[:, S : 2 * S])
+        nc.sync.dma_start(list_c[:], offs3)
+
+        pages = [keep.tile([P, C], F32, name="pp%d" % n) for n in range(2)]
+        for n in range(2):
+            nc.vector.memset(pages[n][:], 0.0)
+
+        w_sb = keep.tile([P, 2 * R], U8, name="w_sb", align_bytes=64)
+        w2_sb = keep.tile([P, R], U32, name="w2_sb", align_bytes=64)
+        nc.vector.tensor_copy(
+            out=landed[:, 0:R].rearrange("p (t c i) -> p c t i", t=PACK, i=16),
+            in_=landed[:, ROW:].rearrange("p (c i t) -> p c t i", t=PACK, i=16),
+        )
+        for q in range(4):
+            nc.sync.dma_start(
+                out=scales[32 * q : 32 * q + 4, :].bitcast(I32),
+                in_=landed[8 * q : 8 * q + 8, 0:ROW].bitcast(I32),
+            )
+        nc.vector.tensor_copy(
+            out=w_sb[:].bitcast(U16).rearrange("p (t c i) -> p c t i", t=PACK, i=8),
+            in_=w_raw[:].bitcast(U16).rearrange("p (c i t) -> p c t i", t=PACK, i=8),
+        )
+        nc.vector.tensor_copy(
+            out=w2_sb[:].rearrange("p (t c i) -> p c t i", t=PACK, i=4),
+            in_=w2_raw[:].rearrange("p (c i t) -> p c t i", t=PACK, i=4),
+        )
+
+        for t in range(2, PACK):
+            xb_sb.append(keep.tile([P, S], F32, name="xb%d" % t, tag="words%d" % (t - 2), align_bytes=64))
+            nc.sync.dma_start(out=xb_sb[t][:], in_=xb_rows[:, t * S : (t + 1) * S])
+
+        picked_a = keep.tile([P, PACK, J], F32, name="picked_a")
+        scaled_a = keep.tile([P, PACK, J], F32, name="scaled_a")
+        prod = keep.tile([P, PACK, J], F32, name="prod")
+        for t in range(PACK):
+            window = xa_sb[t // 2][:, (t % 2) * T : (t % 2 + 1) * T]
+            nc.scalar.activation(picked_a[:, t, :], window.indirect(list_a[:]), COPY)
+            nc.scalar.activation(scaled_a[:, t, :], picked_a[:, t, :], COPY, scale=fk_sb[:, t : t + 1])
+        for t in range(PACK - 1):
+            nc.vector.tensor_tensor(prod[:, t, :], xb_sb[t][:].indirect(list_b[:]), scaled_a[:, t, :], ALU.mult)
+
+        sx_sb = keep.tile([P, J], U32, name="sx_sb", tag="late0", align_bytes=64)
+        wb_sb = keep.tile([P, N], U32, name="wb_sb", tag="late1", align_bytes=64)
+        nc.sync.dma_start(out=sx_sb[:].bitcast(I32), in_=words(sx_words))
+        nc.sync.dma_start(out=wb_sb[:].bitcast(I32), in_=words(wb_words))
+        old_sb = [keep.tile([P, C], F32, name="old%d" % n, tag="page%d" % n) for n in range(2)]
+        for n in range(2):
+            nc.sync.dma_start(out=old_sb[n][:], in_=old[n * P : (n + 1) * P, :])
+
+        q_half = []
+        for h in range(2):
+            bank = psum.tile([P, PACK, HALF], F32, name="q_bank%d" % h)
+            for t in range(PACK):
+                nc.tensor.matmul_mx(
+                    out=bank[:, t, :],
+                    lhsT=w2_sb[:, t * P : (t + 1) * P].bitcast(E5M2),
+                    lhsT_scale=scales[:, W2_SC + t * P : W2_SC + (t + 1) * P],
+                    rhs=sx_sb[:, h * HALF : (h + 1) * HALF].bitcast(E4M3),
+                    rhs_scale=scales[:, SX_SC + h * HALF : SX_SC + (h + 1) * HALF],
+                    start=True, stop=True,
+                )
+            neg_half_q = keep.tile([P, HALF, PACK], F32, name="neg_half_q%d" % h)
+            nc.scalar.activation(neg_half_q[:], bank[:].rearrange("p t j -> p j t"), COPY, scale=-0.5)
+            q_half.append(neg_half_q)
+
+        def cols(h):
+            return slice(h * HALF, (h + 1) * HALF)
+
+        def list_cols(h):
+            return slice(h * LIST_COLS, (h + 1) * LIST_COLS)
+
+        last = PACK - 1
+        u_bf = [keep.tile([P, HALF, PACK], BF16, name="u_bf%d" % h, align_bytes=64) for h in range(2)]
+        for h in range(2):
+            nc.vector.tensor_tensor(
+                prod[:, last, cols(h)], xb_sb[last][:].indirect(list_b[:, list_cols(h)]),
+                scaled_a[:, last, cols(h)], ALU.mult,
+            )
+        a_bank = []
+        for h in range(2):
+            nc.vector.tensor_copy(
+                out=u_bf[h][:].rearrange("p (c i) t -> p c t i", i=4),
+                in_=prod[:, :, cols(h)].rearrange("p t (c i) -> p c t i", i=4),
+            )
+        for h in range(2):
+            codes = keep.tile([P, HALF], U32, name="u_codes%d" % h, align_bytes=64)
+            plane = keep.tile([P, HALF], U8, name="u_plane%d" % h, align_bytes=64)
+            nc.vector.quantize_mx(out=codes[:].bitcast(E4M3), scales=plane[:], in_=u_bf[h][:].rearrange("p j t -> p (j t)"))
+            bank = psum.tile([P, PACK, HALF], F32, name="a_bank%d" % h)
+            for t in range(PACK):
+                nc.tensor.matmul_mx(
+                    out=bank[:, t, :],
+                    lhsT=w_sb[:, 2 * t * P : 2 * (t + 1) * P].bitcast(E2M1),
+                    lhsT_scale=scales[:, W_SC + t * P : W_SC + (t + 1) * P],
+                    rhs=codes[:].bitcast(E4M3),
+                    rhs_scale=plane[:],
+                    start=True, stop=True,
+                )
+            a_bank.append(bank)
+
+        hid_bf = []
+        for h in range(2):
+            a_woven = a_bank[h][:].rearrange("p t j -> p j t")
+            taken = keep.tile([P, HALF, PACK], F32, name="taken%d" % h)
+            nc.vector.scalar_tensor_tensor(taken[:], a_woven, -0.5, q_half[h][:], ALU.mult, ALU.max)
+            hid = keep.tile([P, HALF, PACK], BF16, name="hid%d" % h, align_bytes=64)
+            nc.vector.scalar_tensor_tensor(hid[:], a_woven, 0.0, taken[:], ALU.max, ALU.add)
+            hid_bf.append(hid)
+
+        for h in range(2):
+            codes = keep.tile([P, HALF], U32, name="h_codes%d" % h, align_bytes=64)
+            plane = keep.tile([P, HALF], U8, name="h_plane%d" % h, align_bytes=64)
+            nc.vector.quantize_mx(out=codes[:].bitcast(E5M2), scales=plane[:], in_=hid_bf[h][:].rearrange("p j t -> p (j t)"))
+            bank = psum.tile([P, 2, HALF], F32, name="p_bank%d" % h)
+            for n in range(2):
+                nc.tensor.matmul_mx(
+                    out=bank[:, n, :],
+                    lhsT=wb_sb[:, n * P : (n + 1) * P].bitcast(E5M2),
+                    lhsT_scale=scales[:, WB_SC + n * P : WB_SC + (n + 1) * P],
+                    rhs=codes[:].bitcast(E5M2),
+                    rhs_scale=plane[:],
+                    start=True, stop=True,
+                )
+            p_sb = keep.tile([P, 2, HALF], F32, name="p_sb%d" % h)
+            nc.scalar.copy(p_sb[:], bank[:])
+            for n in range(2):
+                target = pages[n][:].indirect(list_c[:, list_cols(h)])
+                if h == 1 and n == 0:
+                    nc.vector.tensor_copy(target, p_sb[:, n, :])
+                else:
+                    nc.scalar.activation(target, p_sb[:, n, :], COPY)
+
+        for n in range(2):
+            for c0 in range(0, C, OUT_CHUNK):
+                piece = slice(c0, c0 + OUT_CHUNK)
+                res = keep.tile([P, OUT_CHUNK], F32, name="res%d_%d" % (n, c0))
+                nc.vector.scalar_tensor_tensor(res[:], old_sb[n][:, piece], 0.5, pages[n][:, piece], ALU.mult, ALU.add)
+                nc.sync.dma_start(out=out[n * P : (n + 1) * P, piece], in_=res[:])

@@ -21,7 +21,6 @@ P = 128
 PACK = 4
 HALF = J // 2
 LIST_COLS = HALF // 16
-OUT_CHUNK = 512
 
 ROW = R + J
 W_SC, SX_SC, W2_SC, WB_SC = 0, R, ROW, ROW + R
@@ -38,15 +37,14 @@ def tile_list_two_entryproducts_own_smaller_scattered_kernel(
 
         scales = keep.tile([P, 2 * ROW], U8, name="scales", align_bytes=64)
         landed = keep.tile([P, ROW + R], U8, name="landed", align_bytes=64)
-        nc.scalar.dma_start(out=landed[0:32:2, ROW:].bitcast(I32), in_=w_scales[0].bitcast(I32))
-        nc.scalar.dma_start(out=landed[1:32:2, ROW:].bitcast(I32), in_=w2_scales[0].bitcast(I32))
-        nc.scalar.dma_start(out=landed[0:32:2, R:ROW].bitcast(I32), in_=sx_scales[0].bitcast(I32))
-        nc.scalar.dma_start(out=landed[1:32:2, R:ROW].bitcast(I32), in_=wb_scales[0].bitcast(I32))
+        nc.sync.dma_start(out=landed[0:32:2, ROW:].bitcast(I32), in_=w_scales[0].bitcast(I32))
+        nc.sync.dma_start(out=landed[1:32:2, ROW:].bitcast(I32), in_=w2_scales[0].bitcast(I32))
+        nc.sync.dma_start(out=landed[0:32:2, R:ROW].bitcast(I32), in_=sx_scales[0].bitcast(I32))
+        nc.sync.dma_start(out=landed[1:32:2, R:ROW].bitcast(I32), in_=wb_scales[0].bitcast(I32))
         nc.vector.memset(landed[32:64, ROW:].bitcast(I32), 0)
         nc.vector.memset(landed[64:128, ROW:].bitcast(I32), 0)
         nc.vector.memset(scales[:].bitcast(I32), 0)
         fk_sb = keep.tile([P, PACK], F32, name="fk_sb")
-        nc.gpsimd.dma_start(out=fk_sb[:], in_=fk.rearrange("(p t) o -> p (t o)", t=PACK))
 
         list_a = keep.tile([P, J // 16], U16, name="list_a")
         list_b = keep.tile([P, J // 16], U16, name="list_b")
@@ -55,20 +53,27 @@ def tile_list_two_entryproducts_own_smaller_scattered_kernel(
         w2_raw = keep.tile([P, R], U32, name="w2_raw", tag="words1", align_bytes=64)
         xa_rows = xa.rearrange("(p t) c -> p (t c)", t=PACK)
         xb_rows = xb.rearrange("(p t) c -> p (t c)", t=PACK)
-        xa_sb = [keep.tile([P, 2 * T], F32, name="xa%d" % i, tag="page%d" % i) for i in range(2)]
-        xb_sb = [keep.tile([P, S], F32, name="xb%d" % t, tag="late%d" % t, align_bytes=64) for t in range(2)]
+        sx_sb = keep.tile([P, J], U32, name="sx_sb", align_bytes=64)
+        xb_sb = [keep.tile([P, 2 * S], F32, name="xb%d" % i, tag="page%d" % i) for i in range(2)]
+        xa_low = keep.tile([P, 2 * T], F32, name="xa_low")
+        xa_high = [keep.tile([P, T], F32, name="xa%d" % t) for t in range(2, PACK)]
+        xa_plane = [xa_low[:, 0:T], xa_low[:, T : 2 * T], xa_high[0][:], xa_high[1][:]]
+        xb_plane = [xb_sb[t // 2][:, (t % 2) * S : (t % 2 + 1) * S] for t in range(PACK)]
 
         def words(ap):
             return ap[0].rearrange("p n t -> p (n t)").bitcast(I32)
 
-        nc.sync.dma_start(list_a[:], offs)
-        nc.sync.dma_start(out=w_raw[:].bitcast(I32), in_=w_words[0].bitcast(I32))
-        nc.sync.dma_start(out=w2_raw[:].bitcast(I32), in_=words(w2_words))
-        nc.sync.dma_start(out=xa_sb[0][:], in_=xa_rows[:, 0 : 2 * T])
         nc.sync.dma_start(list_b[:], offs2)
-        nc.sync.dma_start(out=xb_sb[0][:], in_=xb_rows[:, 0:S])
-        nc.sync.dma_start(out=xa_sb[1][:], in_=xa_rows[:, 2 * T : 4 * T])
-        nc.sync.dma_start(out=xb_sb[1][:], in_=xb_rows[:, S : 2 * S])
+        nc.sync.dma_start(out=w_raw[:].bitcast(I32), in_=w_words[0].bitcast(I32))
+        nc.sync.dma_start(out=xb_sb[0][:], in_=xb_rows[:, 0 : 2 * S])
+        nc.sync.dma_start(out=xa_low[:], in_=xa_rows[:, 0 : 2 * T])
+        nc.sync.dma_start(list_a[:], offs)
+        nc.sync.dma_start(out=fk_sb[:], in_=fk.rearrange("(p t) o -> p (t o)", t=PACK))
+        nc.sync.dma_start(out=w2_raw[:].bitcast(I32), in_=words(w2_words))
+        nc.sync.dma_start(out=xb_sb[1][:], in_=xb_rows[:, 2 * S : 4 * S])
+        for t in range(2, PACK):
+            nc.sync.dma_start(out=xa_plane[t], in_=xa_rows[:, t * T : (t + 1) * T])
+        nc.sync.dma_start(out=sx_sb[:].bitcast(I32), in_=words(sx_words))
         nc.sync.dma_start(list_c[:], offs3)
 
         pages = [keep.tile([P, C], F32, name="pp%d" % n) for n in range(2)]
@@ -82,7 +87,7 @@ def tile_list_two_entryproducts_own_smaller_scattered_kernel(
             in_=landed[:, ROW:].rearrange("p (c i t) -> p c t i", t=PACK, i=16),
         )
         for q in range(4):
-            nc.sync.dma_start(
+            (nc.gpsimd if q < 2 else nc.sync).dma_start(
                 out=scales[32 * q : 32 * q + 4, :].bitcast(I32),
                 in_=landed[8 * q : 8 * q + 8, 0:ROW].bitcast(I32),
             )
@@ -95,24 +100,45 @@ def tile_list_two_entryproducts_own_smaller_scattered_kernel(
             in_=w2_raw[:].rearrange("p (c i t) -> p c t i", t=PACK, i=4),
         )
 
-        for t in range(2, PACK):
-            xb_sb.append(keep.tile([P, S], F32, name="xb%d" % t, tag="words%d" % (t - 2), align_bytes=64))
-            nc.sync.dma_start(out=xb_sb[t][:], in_=xb_rows[:, t * S : (t + 1) * S])
-
-        picked_a = keep.tile([P, PACK, J], F32, name="picked_a")
-        scaled_a = keep.tile([P, PACK, J], F32, name="scaled_a")
-        prod = keep.tile([P, PACK, J], F32, name="prod")
-        for t in range(PACK):
-            window = xa_sb[t // 2][:, (t % 2) * T : (t % 2 + 1) * T]
-            nc.scalar.activation(picked_a[:, t, :], window.indirect(list_a[:]), COPY)
-            nc.scalar.activation(scaled_a[:, t, :], picked_a[:, t, :], COPY, scale=fk_sb[:, t : t + 1])
-        for t in range(PACK - 1):
-            nc.vector.tensor_tensor(prod[:, t, :], xb_sb[t][:].indirect(list_b[:]), scaled_a[:, t, :], ALU.mult)
-
-        sx_sb = keep.tile([P, J], U32, name="sx_sb", tag="late0", align_bytes=64)
-        wb_sb = keep.tile([P, N], U32, name="wb_sb", tag="late1", align_bytes=64)
-        nc.sync.dma_start(out=sx_sb[:].bitcast(I32), in_=words(sx_words))
+        wb_sb = keep.tile([P, N], U32, name="wb_sb", tag="words0", align_bytes=64)
         nc.sync.dma_start(out=wb_sb[:].bitcast(I32), in_=words(wb_words))
+
+        def cols(h):
+            return slice(h * HALF, (h + 1) * HALF)
+
+        def list_cols(h):
+            return slice(h * LIST_COLS, (h + 1) * LIST_COLS)
+
+        last = PACK - 1
+        picked_a = keep.tile([P, PACK, J], F32, name="picked_a")
+        picked_b = keep.tile([P, last, J], F32, name="picked_b")
+        b_slot = [0, 1, 0, 2]
+        prod = keep.tile([P, PACK, J], F32, name="prod", tag="words1", align_bytes=64)
+
+        def multiply(t, js):
+            nc.vector.scalar_tensor_tensor(
+                prod[:, t, js], picked_a[:, t, js], fk_sb[:, t : t + 1], picked_b[:, b_slot[t], js], ALU.mult, ALU.mult
+            )
+
+        def pick_a(t, js, list_js):
+            nc.scalar.activation(picked_a[:, t, js], xa_plane[t].indirect(list_a[:, list_js]), COPY)
+
+        def pick_b_on_scalar(t):
+            nc.scalar.activation(picked_b[:, b_slot[t], :], xb_plane[t].indirect(list_b[:]), COPY)
+
+        whole, whole_list = slice(0, J), slice(0, J // 16)
+        for t in range(2):
+            pick_b_on_scalar(t)
+        for t in range(2):
+            pick_a(t, whole, whole_list)
+            multiply(t, whole)
+        pick_b_on_scalar(last)
+        nc.vector.tensor_copy(picked_b[:, b_slot[2], :], xb_plane[2].indirect(list_b[:]))
+        pick_a(2, whole, whole_list)
+        multiply(2, whole)
+        for h in range(2):
+            pick_a(last, cols(h), list_cols(h))
+
         old_sb = [keep.tile([P, C], F32, name="old%d" % n, tag="page%d" % n) for n in range(2)]
         for n in range(2):
             nc.sync.dma_start(out=old_sb[n][:], in_=old[n * P : (n + 1) * P, :])
@@ -133,76 +159,80 @@ def tile_list_two_entryproducts_own_smaller_scattered_kernel(
             nc.scalar.activation(neg_half_q[:], bank[:].rearrange("p t j -> p j t"), COPY, scale=-0.5)
             q_half.append(neg_half_q)
 
-        def cols(h):
-            return slice(h * HALF, (h + 1) * HALF)
-
-        def list_cols(h):
-            return slice(h * LIST_COLS, (h + 1) * LIST_COLS)
-
-        last = PACK - 1
         u_bf = [keep.tile([P, HALF, PACK], BF16, name="u_bf%d" % h, align_bytes=64) for h in range(2)]
-        for h in range(2):
-            nc.vector.tensor_tensor(
-                prod[:, last, cols(h)], xb_sb[last][:].indirect(list_b[:, list_cols(h)]),
-                scaled_a[:, last, cols(h)], ALU.mult,
-            )
-        a_bank = []
-        for h in range(2):
+        a_bank = [psum.tile([P, PACK, HALF], F32, name="a_bank%d" % h) for h in range(2)]
+
+        def weave_u(h):
             nc.vector.tensor_copy(
                 out=u_bf[h][:].rearrange("p (c i) t -> p c t i", i=4),
                 in_=prod[:, :, cols(h)].rearrange("p t (c i) -> p c t i", i=4),
             )
-        for h in range(2):
+
+        def first_product(h):
             codes = keep.tile([P, HALF], U32, name="u_codes%d" % h, align_bytes=64)
             plane = keep.tile([P, HALF], U8, name="u_plane%d" % h, align_bytes=64)
             nc.vector.quantize_mx(out=codes[:].bitcast(E4M3), scales=plane[:], in_=u_bf[h][:].rearrange("p j t -> p (j t)"))
-            bank = psum.tile([P, PACK, HALF], F32, name="a_bank%d" % h)
             for t in range(PACK):
                 nc.tensor.matmul_mx(
-                    out=bank[:, t, :],
+                    out=a_bank[h][:, t, :],
                     lhsT=w_sb[:, 2 * t * P : 2 * (t + 1) * P].bitcast(E2M1),
                     lhsT_scale=scales[:, W_SC + t * P : W_SC + (t + 1) * P],
                     rhs=codes[:].bitcast(E4M3),
                     rhs_scale=plane[:],
                     start=True, stop=True,
                 )
-            a_bank.append(bank)
 
-        hid_bf = []
-        for h in range(2):
+        multiply(last, cols(0))
+        weave_u(0)
+        multiply(last, cols(1))
+        first_product(0)
+        weave_u(1)
+        first_product(1)
+
+        taken = [keep.tile([P, HALF, PACK], F32, name="taken%d" % h) for h in range(2)]
+        hid_bf = [keep.tile([P, HALF, PACK], BF16, name="hid%d" % h, align_bytes=64) for h in range(2)]
+        p_bank = [psum.tile([P, 2, HALF], F32, name="p_bank%d" % h) for h in range(2)]
+        p_sb = [keep.tile([P, 2, HALF], F32, name="p_sb%d" % h) for h in range(2)]
+
+        def smaller(h):
             a_woven = a_bank[h][:].rearrange("p t j -> p j t")
-            taken = keep.tile([P, HALF, PACK], F32, name="taken%d" % h)
-            nc.vector.scalar_tensor_tensor(taken[:], a_woven, -0.5, q_half[h][:], ALU.mult, ALU.max)
-            hid = keep.tile([P, HALF, PACK], BF16, name="hid%d" % h, align_bytes=64)
-            nc.vector.scalar_tensor_tensor(hid[:], a_woven, 0.0, taken[:], ALU.max, ALU.add)
-            hid_bf.append(hid)
+            nc.vector.scalar_tensor_tensor(taken[h][:], a_woven, -0.5, q_half[h][:], ALU.mult, ALU.max)
 
-        for h in range(2):
+        def hidden(h):
+            a_woven = a_bank[h][:].rearrange("p t j -> p j t")
+            nc.vector.scalar_tensor_tensor(hid_bf[h][:], a_woven, 0.0, taken[h][:], ALU.max, ALU.add)
+
+        def second_product(h):
             codes = keep.tile([P, HALF], U32, name="h_codes%d" % h, align_bytes=64)
             plane = keep.tile([P, HALF], U8, name="h_plane%d" % h, align_bytes=64)
             nc.vector.quantize_mx(out=codes[:].bitcast(E5M2), scales=plane[:], in_=hid_bf[h][:].rearrange("p j t -> p (j t)"))
-            bank = psum.tile([P, 2, HALF], F32, name="p_bank%d" % h)
             for n in range(2):
                 nc.tensor.matmul_mx(
-                    out=bank[:, n, :],
+                    out=p_bank[h][:, n, :],
                     lhsT=wb_sb[:, n * P : (n + 1) * P].bitcast(E5M2),
                     lhsT_scale=scales[:, WB_SC + n * P : WB_SC + (n + 1) * P],
                     rhs=codes[:].bitcast(E5M2),
                     rhs_scale=plane[:],
                     start=True, stop=True,
                 )
-            p_sb = keep.tile([P, 2, HALF], F32, name="p_sb%d" % h)
-            nc.scalar.copy(p_sb[:], bank[:])
-            for n in range(2):
-                target = pages[n][:].indirect(list_c[:, list_cols(h)])
-                if h == 1 and n == 0:
-                    nc.vector.tensor_copy(target, p_sb[:, n, :])
-                else:
-                    nc.scalar.activation(target, p_sb[:, n, :], COPY)
 
-        for n in range(2):
-            for c0 in range(0, C, OUT_CHUNK):
-                piece = slice(c0, c0 + OUT_CHUNK)
-                res = keep.tile([P, OUT_CHUNK], F32, name="res%d_%d" % (n, c0))
-                nc.vector.scalar_tensor_tensor(res[:], old_sb[n][:, piece], 0.5, pages[n][:, piece], ALU.mult, ALU.add)
-                nc.sync.dma_start(out=out[n * P : (n + 1) * P, piece], in_=res[:])
+        def place(h):
+            nc.vector.tensor_copy(pages[0][:].indirect(list_c[:, list_cols(h)]), p_sb[h][:, 0, :])
+            nc.scalar.activation(pages[1][:].indirect(list_c[:, list_cols(h)]), p_sb[h][:, 1, :], COPY)
+
+        smaller(0)
+        hidden(0)
+        smaller(1)
+        second_product(0)
+        hidden(1)
+        second_product(1)
+        nc.scalar.copy(p_sb[0][:], p_bank[0][:])
+        place(0)
+        nc.vector.tensor_copy(p_sb[1][:], p_bank[1][:])
+        place(1)
+
+        for n, c0, c1 in ((0, 0, 512), (0, 512, 1024), (1, 0, 512), (1, 512, 768), (1, 768, 1024)):
+            piece = slice(c0, c1)
+            res = keep.tile([P, c1 - c0], F32, name="res%d_%d" % (n, c0))
+            nc.vector.scalar_tensor_tensor(res[:], old_sb[n][:, piece], 0.5, pages[n][:, piece], ALU.mult, ALU.add)
+            nc.sync.dma_start(out=out[n * P : (n + 1) * P, piece], in_=res[:])

@@ -35,6 +35,10 @@ def tile_list_two_entryproducts_own_smaller_scattered_kernel(
         keep = ctx.enter_context(tc.tile_pool(name="keep", bufs=1))
         psum = ctx.enter_context(tc.psum_pool(name="psum", bufs=1))
 
+        warm = keep.tile([P, 16], F32, name="warm")
+        nc.vector.memset(warm[:, 0:1], 0.0)
+        nc.scalar.activation(warm[:, 8:9], warm[:, 0:1], COPY)
+
         scales = keep.tile([P, 2 * ROW], U8, name="scales", align_bytes=64)
         landed = keep.tile([P, ROW + R], U8, name="landed", align_bytes=64)
         nc.sync.dma_start(out=landed[0:32:2, ROW:].bitcast(I32), in_=w_scales[0].bitcast(I32))
@@ -45,6 +49,7 @@ def tile_list_two_entryproducts_own_smaller_scattered_kernel(
         nc.vector.memset(landed[64:128, ROW:].bitcast(I32), 0)
         nc.vector.memset(scales[:].bitcast(I32), 0)
         fk_sb = keep.tile([P, PACK], F32, name="fk_sb")
+        nc.gpsimd.dma_start(out=fk_sb[:], in_=fk.rearrange("(p t) o -> p (t o)", t=PACK))
 
         list_a = keep.tile([P, J // 16], U16, name="list_a")
         list_b = keep.tile([P, J // 16], U16, name="list_b")
@@ -56,7 +61,7 @@ def tile_list_two_entryproducts_own_smaller_scattered_kernel(
         sx_sb = keep.tile([P, J], U32, name="sx_sb", align_bytes=64)
         xb_sb = [keep.tile([P, 2 * S], F32, name="xb%d" % i, tag="page%d" % i) for i in range(2)]
         xa_low = keep.tile([P, 2 * T], F32, name="xa_low")
-        xa_high = [keep.tile([P, T], F32, name="xa%d" % t) for t in range(2, PACK)]
+        xa_high = [keep.tile([P, T], F32, name="xa%d" % t, tag="xa%d" % t) for t in range(2, PACK)]
         xa_plane = [xa_low[:, 0:T], xa_low[:, T : 2 * T], xa_high[0][:], xa_high[1][:]]
         xb_plane = [xb_sb[t // 2][:, (t % 2) * S : (t % 2 + 1) * S] for t in range(PACK)]
 
@@ -68,7 +73,6 @@ def tile_list_two_entryproducts_own_smaller_scattered_kernel(
         nc.sync.dma_start(out=xb_sb[0][:], in_=xb_rows[:, 0 : 2 * S])
         nc.sync.dma_start(out=xa_low[:], in_=xa_rows[:, 0 : 2 * T])
         nc.sync.dma_start(list_a[:], offs)
-        nc.sync.dma_start(out=fk_sb[:], in_=fk.rearrange("(p t) o -> p (t o)", t=PACK))
         nc.sync.dma_start(out=w2_raw[:].bitcast(I32), in_=words(w2_words))
         nc.sync.dma_start(out=xb_sb[1][:], in_=xb_rows[:, 2 * S : 4 * S])
         for t in range(2, PACK):
@@ -143,7 +147,7 @@ def tile_list_two_entryproducts_own_smaller_scattered_kernel(
         for n in range(2):
             nc.sync.dma_start(out=old_sb[n][:], in_=old[n * P : (n + 1) * P, :])
 
-        q_half = []
+        neg_half_q = keep.tile([P, 2, HALF, PACK], F32, name="neg_half_q", tag="xa%d" % last)
         for h in range(2):
             bank = psum.tile([P, PACK, HALF], F32, name="q_bank%d" % h)
             for t in range(PACK):
@@ -155,14 +159,13 @@ def tile_list_two_entryproducts_own_smaller_scattered_kernel(
                     rhs_scale=scales[:, SX_SC + h * HALF : SX_SC + (h + 1) * HALF],
                     start=True, stop=True,
                 )
-            neg_half_q = keep.tile([P, HALF, PACK], F32, name="neg_half_q%d" % h)
-            nc.scalar.activation(neg_half_q[:], bank[:].rearrange("p t j -> p j t"), COPY, scale=-0.5)
-            q_half.append(neg_half_q)
+            nc.scalar.activation(neg_half_q[:, h], bank[:].rearrange("p t j -> p j t"), COPY, scale=-0.5)
 
-        u_bf = [keep.tile([P, HALF, PACK], BF16, name="u_bf%d" % h, align_bytes=64) for h in range(2)]
+        u_bf = {}
         a_bank = [psum.tile([P, PACK, HALF], F32, name="a_bank%d" % h) for h in range(2)]
 
         def weave_u(h):
+            u_bf.setdefault(h, keep.tile([P, HALF, PACK], BF16, name="u_bf", align_bytes=64))
             nc.vector.tensor_copy(
                 out=u_bf[h][:].rearrange("p (c i) t -> p c t i", i=4),
                 in_=prod[:, :, cols(h)].rearrange("p t (c i) -> p c t i", i=4),
@@ -190,15 +193,16 @@ def tile_list_two_entryproducts_own_smaller_scattered_kernel(
         first_product(1)
 
         taken = [keep.tile([P, HALF, PACK], F32, name="taken%d" % h) for h in range(2)]
-        hid_bf = [keep.tile([P, HALF, PACK], BF16, name="hid%d" % h, align_bytes=64) for h in range(2)]
+        hid_bf = {}
         p_bank = [psum.tile([P, 2, HALF], F32, name="p_bank%d" % h) for h in range(2)]
         p_sb = [keep.tile([P, 2, HALF], F32, name="p_sb%d" % h) for h in range(2)]
 
         def smaller(h):
             a_woven = a_bank[h][:].rearrange("p t j -> p j t")
-            nc.vector.scalar_tensor_tensor(taken[h][:], a_woven, -0.5, q_half[h][:], ALU.mult, ALU.max)
+            nc.vector.scalar_tensor_tensor(taken[h][:], a_woven, -0.5, neg_half_q[:, h], ALU.mult, ALU.max)
 
         def hidden(h):
+            hid_bf.setdefault(h, keep.tile([P, HALF, PACK], BF16, name="hid_bf", align_bytes=64))
             a_woven = a_bank[h][:].rearrange("p t j -> p j t")
             nc.vector.scalar_tensor_tensor(hid_bf[h][:], a_woven, 0.0, taken[h][:], ALU.max, ALU.add)
 
@@ -228,7 +232,7 @@ def tile_list_two_entryproducts_own_smaller_scattered_kernel(
         second_product(1)
         nc.scalar.copy(p_sb[0][:], p_bank[0][:])
         place(0)
-        nc.vector.tensor_copy(p_sb[1][:], p_bank[1][:])
+        nc.scalar.copy(p_sb[1][:], p_bank[1][:])
         place(1)
 
         for n, c0, c1 in ((0, 0, 512), (0, 512, 1024), (1, 0, 512), (1, 512, 768), (1, 768, 1024)):

@@ -49,7 +49,6 @@ def tile_list_two_entryproducts_own_smaller_scattered_kernel(
         nc.vector.memset(landed[64:128, ROW:].bitcast(I32), 0)
         nc.vector.memset(scales[:].bitcast(I32), 0)
         fk_sb = keep.tile([P, PACK], F32, name="fk_sb")
-        nc.gpsimd.dma_start(out=fk_sb[:], in_=fk.rearrange("(p t) o -> p (t o)", t=PACK))
 
         list_a = keep.tile([P, J // 16], U16, name="list_a")
         list_b = keep.tile([P, J // 16], U16, name="list_b")
@@ -73,6 +72,7 @@ def tile_list_two_entryproducts_own_smaller_scattered_kernel(
         nc.sync.dma_start(out=xb_sb[0][:], in_=xb_rows[:, 0 : 2 * S])
         nc.sync.dma_start(out=xa_low[:], in_=xa_rows[:, 0 : 2 * T])
         nc.sync.dma_start(list_a[:], offs)
+        nc.sync.dma_start(out=fk_sb[:], in_=fk.rearrange("(p t) o -> p (t o)", t=PACK))
         nc.sync.dma_start(out=w2_raw[:].bitcast(I32), in_=words(w2_words))
         nc.sync.dma_start(out=xb_sb[1][:], in_=xb_rows[:, 2 * S : 4 * S])
         for t in range(2, PACK):
@@ -91,7 +91,7 @@ def tile_list_two_entryproducts_own_smaller_scattered_kernel(
             in_=landed[:, ROW:].rearrange("p (c i t) -> p c t i", t=PACK, i=16),
         )
         for q in range(4):
-            (nc.gpsimd if q < 2 else nc.sync).dma_start(
+            nc.sync.dma_start(
                 out=scales[32 * q : 32 * q + 4, :].bitcast(I32),
                 in_=landed[8 * q : 8 * q + 8, 0:ROW].bitcast(I32),
             )

from contextlib import ExitStack

import concourse.mybir as mybir

K, T, J, S, R, F, N, C = 512, 512, 256, 512, 512, 512, 256, 1024
FLOPS = 2 * (K * R * J + F * R * J + R * N * J)

F32 = mybir.dt.float32
BF16 = mybir.dt.bfloat16
I32 = mybir.dt.int32
U32 = mybir.dt.uint32
U16 = mybir.dt.uint16
U8 = mybir.dt.uint8
E4M3 = mybir.dt.float8_e4m3fn_x4
E5M2 = mybir.dt.float8_e5m2_x4
E2M1 = mybir.dt.float4_e2m1fn_x4
ALU = mybir.AluOpType
COPY = mybir.ActivationFunctionType.Copy

P = 128
PACK = 4
HALF = J // 2
LIST_COLS = HALF // 16

ROW = R + J
W_SC, SX_SC, W2_SC, WB_SC = 0, R, ROW, ROW + R


def tile_list_two_entryproducts_own_smaller_scattered_kernel(
    tc, xa, xb, fk, w_words, w_scales, sx_words, sx_scales, w2_words, w2_scales,
    wb_words, wb_scales, old, offs, offs2, offs3, out,
):
    nc = tc.nc
    with ExitStack() as ctx:
        keep = ctx.enter_context(tc.tile_pool(name="keep", bufs=1))
        psum = ctx.enter_context(tc.psum_pool(name="psum", bufs=1))

        warm = keep.tile([P, 16], F32, name="warm")
        nc.vector.memset(warm[:, 0:1], 0.0)
        nc.scalar.activation(warm[:, 8:9], warm[:, 0:1], COPY)

        scales = keep.tile([P, 2 * ROW], U8, name="scales", align_bytes=64)
        landed = keep.tile([P, ROW + R], U8, name="landed", align_bytes=64)
        nc.sync.dma_start(out=landed[0:32:2, ROW:].bitcast(I32), in_=w_scales[0].bitcast(I32))
        nc.sync.dma_start(out=landed[1:32:2, ROW:].bitcast(I32), in_=w2_scales[0].bitcast(I32))
        nc.sync.dma_start(out=landed[0:32:2, R:ROW].bitcast(I32), in_=sx_scales[0].bitcast(I32))
        nc.sync.dma_start(out=landed[1:32:2, R:ROW].bitcast(I32), in_=wb_scales[0].bitcast(I32))
        nc.vector.memset(landed[32:64, ROW:].bitcast(I32), 0)
        nc.vector.memset(landed[64:128, ROW:].bitcast(I32), 0)
        nc.vector.memset(scales[:].bitcast(I32), 0)
        fk_sb = keep.tile([P, PACK], F32, name="fk_sb")

        list_a = keep.tile([P, J // 16], U16, name="list_a")
        list_b = keep.tile([P, J // 16], U16, name="list_b")
        list_c = keep.tile([P, J // 16], U16, name="list_c")
        w_raw = keep.tile([P, 2 * R], U8, name="w_raw", tag="words0", align_bytes=64)
        w2_raw = keep.tile([P, R], U32, name="w2_raw", tag="words1", align_bytes=64)
        xa_rows = xa.rearrange("(p t) c -> p (t c)", t=PACK)
        xb_rows = xb.rearrange("(p t) c -> p (t c)", t=PACK)
        sx_sb = keep.tile([P, J], U32, name="sx_sb", align_bytes=64)
        xb_sb = [keep.tile([P, 2 * S], F32, name="xb%d" % i, tag="page%d" % i) for i in range(2)]
        xa_low = keep.tile([P, 2 * T], F32, name="xa_low")
        xa_high = [keep.tile([P, T], F32, name="xa%d" % t, tag="xa%d" % t) for t in range(2, PACK)]
        xa_plane = [xa_low[:, 0:T], xa_low[:, T : 2 * T], xa_high[0][:], xa_high[1][:]]
        xb_plane = [xb_sb[t // 2][:, (t % 2) * S : (t % 2 + 1) * S] for t in range(PACK)]

        def words(ap):
            return ap[0].rearrange("p n t -> p (n t)").bitcast(I32)

        nc.sync.dma_start(list_b[:], offs2)
        nc.sync.dma_start(out=w_raw[:].bitcast(I32), in_=w_words[0].bitcast(I32))
        nc.sync.dma_start(out=xb_sb[0][:], in_=xb_rows[:, 0 : 2 * S])
        nc.sync.dma_start(out=xa_low[:], in_=xa_rows[:, 0 : 2 * T])
        nc.sync.dma_start(list_a[:], offs)
        nc.sync.dma_start(out=fk_sb[:], in_=fk.rearrange("(p t) o -> p (t o)", t=PACK))
        nc.sync.dma_start(out=w2_raw[:].bitcast(I32), in_=words(w2_words))
        nc.sync.dma_start(out=xb_sb[1][:], in_=xb_rows[:, 2 * S : 4 * S])
        for t in range(2, PACK):
            nc.sync.dma_start(out=xa_plane[t], in_=xa_rows[:, t * T : (t + 1) * T])
        nc.sync.dma_start(out=sx_sb[:].bitcast(I32), in_=words(sx_words))
        nc.sync.dma_start(list_c[:], offs3)

        pages = [keep.tile([P, C], F32, name="pp%d" % n) for n in range(2)]
        for n in range(2):
            nc.vector.memset(pages[n][:], 0.0)

        w_sb = keep.tile([P, 2 * R], U8, name="w_sb", align_bytes=64)
        w2_sb = keep.tile([P, R], U32, name="w2_sb", align_bytes=64)
        nc.vector.tensor_copy(
            out=landed[:, 0:R].rearrange("p (t c i) -> p c t i", t=PACK, i=16),
            in_=landed[:, ROW:].rearrange("p (c i t) -> p c t i", t=PACK, i=16),
        )
        for q in range(4):
            nc.sync.dma_start(
                out=scales[32 * q : 32 * q + 4, :].bitcast(I32),
                in_=landed[8 * q : 8 * q + 8, 0:ROW].bitcast(I32),
            )
        nc.vector.tensor_copy(
            out=w_sb[:].bitcast(U16).rearrange("p (t c i) -> p c t i", t=PACK, i=8),
            in_=w_raw[:].bitcast(U16).rearrange("p (c i t) -> p c t i", t=PACK, i=8),
        )
        nc.vector.tensor_copy(
            out=w2_sb[:].rearrange("p (t c i) -> p c t i", t=PACK, i=4),
            in_=w2_raw[:].rearrange("p (c i t) -> p c t i", t=PACK, i=4),
        )

        wb_sb = keep.tile([P, N], U32, name="wb_sb", tag="words0", align_bytes=64)
        nc.sync.dma_start(out=wb_sb[:].bitcast(I32), in_=words(wb_words))

        def cols(h):
            return slice(h * HALF, (h + 1) * HALF)

        def list_cols(h):
            return slice(h * LIST_COLS, (h + 1) * LIST_COLS)

        last = PACK - 1
        picked_a = keep.tile([P, PACK, J], F32, name="picked_a")
        picked_b = keep.tile([P, last, J], F32, name="picked_b")
        b_slot = [0, 1, 0, 2]
        prod = keep.tile([P, PACK, J], F32, name="prod", tag="words1", align_bytes=64)

        def multiply(t, js):
            nc.vector.scalar_tensor_tensor(
                prod[:, t, js], picked_a[:, t, js], fk_sb[:, t : t + 1], picked_b[:, b_slot[t], js], ALU.mult, ALU.mult
            )

        def pick_a(t, js, list_js):
            nc.scalar.activation(picked_a[:, t, js], xa_plane[t].indirect(list_a[:, list_js]), COPY)

        def pick_b_on_scalar(t):
            nc.scalar.activation(picked_b[:, b_slot[t], :], xb_plane[t].indirect(list_b[:]), COPY)

        whole, whole_list = slice(0, J), slice(0, J // 16)
        for t in range(2):
            pick_b_on_scalar(t)
        for t in range(2):
            pick_a(t, whole, whole_list)
            multiply(t, whole)
        pick_b_on_scalar(last)
        nc.vector.tensor_copy(picked_b[:, b_slot[2], :], xb_plane[2].indirect(list_b[:]))
        pick_a(2, whole, whole_list)
        multiply(2, whole)
        for h in range(2):
            pick_a(last, cols(h), list_cols(h))

        old_sb = [keep.tile([P, C], F32, name="old%d" % n, tag="page%d" % n) for n in range(2)]
        for n in range(2):
            nc.sync.dma_start(out=old_sb[n][:], in_=old[n * P : (n + 1) * P, :])

        neg_half_q = keep.tile([P, 2, HALF, PACK], F32, name="neg_half_q", tag="xa%d" % last)
        for h in range(2):
            bank = psum.tile([P, PACK, HALF], F32, name="q_bank%d" % h)
            for t in range(PACK):
                nc.tensor.matmul_mx(
                    out=bank[:, t, :],
                    lhsT=w2_sb[:, t * P : (t + 1) * P].bitcast(E5M2),
                    lhsT_scale=scales[:, W2_SC + t * P : W2_SC + (t + 1) * P],
                    rhs=sx_sb[:, h * HALF : (h + 1) * HALF].bitcast(E4M3),
                    rhs_scale=scales[:, SX_SC + h * HALF : SX_SC + (h + 1) * HALF],
                    start=True, stop=True,
                )
            nc.scalar.activation(neg_half_q[:, h], bank[:].rearrange("p t j -> p j t"), COPY, scale=-0.5)

        u_bf = {}
        a_bank = [psum.tile([P, PACK, HALF], F32, name="a_bank%d" % h) for h in range(2)]

        def weave_u(h):
            u_bf.setdefault(h, keep.tile([P, HALF, PACK], BF16, name="u_bf", align_bytes=64))
            nc.vector.tensor_copy(
                out=u_bf[h][:].rearrange("p (c i) t -> p c t i", i=4),
                in_=prod[:, :, cols(h)].rearrange("p t (c i) -> p c t i", i=4),
            )

        def first_product(h):
            codes = keep.tile([P, HALF], U32, name="u_codes%d" % h, align_bytes=64)
            plane = keep.tile([P, HALF], U8, name="u_plane%d" % h, align_bytes=64)
            nc.vector.quantize_mx(out=codes[:].bitcast(E4M3), scales=plane[:], in_=u_bf[h][:].rearrange("p j t -> p (j t)"))
            for t in range(PACK):
                nc.tensor.matmul_mx(
                    out=a_bank[h][:, t, :],
                    lhsT=w_sb[:, 2 * t * P : 2 * (t + 1) * P].bitcast(E2M1),
                    lhsT_scale=scales[:, W_SC + t * P : W_SC + (t + 1) * P],
                    rhs=codes[:].bitcast(E4M3),
                    rhs_scale=plane[:],
                    start=True, stop=True,
                )

        multiply(last, cols(0))
        weave_u(0)
        multiply(last, cols(1))
        first_product(0)
        weave_u(1)
        first_product(1)

        taken = [keep.tile([P, HALF, PACK], F32, name="taken%d" % h) for h in range(2)]
        hid_bf = {}
        p_bank = [psum.tile([P, 2, HALF], F32, name="p_bank%d" % h) for h in range(2)]
        p_sb = [keep.tile([P, 2, HALF], F32, name="p_sb%d" % h) for h in range(2)]

        def smaller(h):
            a_woven = a_bank[h][:].rearrange("p t j -> p j t")
            nc.vector.scalar_tensor_tensor(taken[h][:], a_woven, -0.5, neg_half_q[:, h], ALU.mult, ALU.max)

        def hidden(h):
            hid_bf.setdefault(h, keep.tile([P, HALF, PACK], BF16, name="hid_bf", align_bytes=64))
            a_woven = a_bank[h][:].rearrange("p t j -> p j t")
            nc.vector.scalar_tensor_tensor(hid_bf[h][:], a_woven, 0.0, taken[h][:], ALU.max, ALU.add)

        def second_product(h):
            codes = keep.tile([P, HALF], U32, name="h_codes%d" % h, align_bytes=64)
            plane = keep.tile([P, HALF], U8, name="h_plane%d" % h, align_bytes=64)
            nc.vector.quantize_mx(out=codes[:].bitcast(E5M2), scales=plane[:], in_=hid_bf[h][:].rearrange("p j t -> p (j t)"))
            for n in range(2):
                nc.tensor.matmul_mx(
                    out=p_bank[h][:, n, :],
                    lhsT=wb_sb[:, n * P : (n + 1) * P].bitcast(E5M2),
                    lhsT_scale=scales[:, WB_SC + n * P : WB_SC + (n + 1) * P],
                    rhs=codes[:].bitcast(E5M2),
                    rhs_scale=plane[:],
                    start=True, stop=True,
                )

        def place(h):
            nc.vector.tensor_copy(pages[0][:].indirect(list_c[:, list_cols(h)]), p_sb[h][:, 0, :])
            nc.scalar.activation(pages[1][:].indirect(list_c[:, list_cols(h)]), p_sb[h][:, 1, :], COPY)

        smaller(0)
        hidden(0)
        smaller(1)
        second_product(0)
        hidden(1)
        second_product(1)
        nc.scalar.copy(p_sb[0][:], p_bank[0][:])
        place(0)
        nc.scalar.copy(p_sb[1][:], p_bank[1][:])
        place(1)

        for n, c0, c1 in ((0, 0, 512), (0, 512, 1024), (1, 0, 512), (1, 512, 768), (1, 768, 1024)):
            piece = slice(c0, c1)
            res = keep.tile([P, c1 - c0], F32, name="res%d_%d" % (n, c0))
            nc.vector.scalar_tensor_tensor(res[:], old_sb[n][:, piece], 0.5, pages[n][:, piece], ALU.mult, ALU.add)
            nc.sync.dma_start(out=out[n * P : (n + 1) * P, piece], in_=res[:])
